import numpy as np
import ml_dtypes


def mxq(x, axis, fmt="e4m3"):
    dtype, down = {"e4m3": (ml_dtypes.float8_e4m3fn, 7), "e5m2": (ml_dtypes.float8_e5m2, 14)}[fmt]
    v = np.moveaxis(np.asarray(x, np.float32).astype(ml_dtypes.bfloat16).astype(np.float64), axis, -1)
    blocks = v.reshape(v.shape[:-1] + (-1, 32))
    amax = np.abs(blocks).max(-1, keepdims=True)
    byte = np.maximum(np.where(amax > 0, np.frexp(amax)[1] - 1 + 127, 0) - down, 1)
    scale = np.exp2(byte - 127.0)
    codes = (blocks / scale).astype(np.float32).astype(dtype).astype(np.float64)
    return np.moveaxis((codes * scale).reshape(v.shape), -1, axis)


WIDE = False


def mx_kscale(k):
    if not WIDE:
        return np.ones(k)
    levels = np.array([10, -10, 5, -5, 0])
    if k % 512:
        return np.exp2(np.random.permutation(np.resize(levels, k // 32))).repeat(32)
    a = np.empty((k // 512, 16))
    for p in range(k // 512):
        a[p, :8] = np.random.permutation(np.resize(levels, 8))
        for g in range(8):
            far = levels[np.abs(levels - a[p, g]) >= 10]
            a[p, g + 8] = far[np.random.randint(len(far))]
    return np.exp2(a.ravel()).repeat(32)


def f64(x):
    return np.asarray(x).astype(np.float64)


def striped(idx):
    return np.tile(idx.reshape(-1, 16).T, (8, 1)).astype(np.uint16)


def unstriped(offs):
    return offs[:16].T.reshape(-1).astype(np.int64)


E2M1 = np.array([0.0, 0.5, 1.0, 1.5, 2.0, 3.0, 4.0, 6.0, -0.0, -0.5, -1.0, -1.5, -2.0, -3.0, -4.0, -6.0])


def pack_weight(w, fmt):
    k, n = w.shape
    w = f64(np.asarray(w, np.float32).astype(ml_dtypes.bfloat16)).reshape(k // 32, 32, n)
    amax = np.abs(w).max(1)
    if fmt == "e4m3":
        byte = np.frexp(amax)[1] - 1 + 127 - 7
    else:
        mant, ex = np.frexp(amax / 6.0)
        byte = np.where(mant > 0.5, ex, ex - 1) + 127
    byte = np.clip(np.where(amax > 0, byte, 1), 1, 254)
    scaled = (w * np.exp2(127.0 - byte)[:, None, :]).reshape(k, n).astype(np.float32)
    by_word = np.ascontiguousarray(scaled.reshape(k // 512, 128, 4, n).transpose(0, 1, 3, 2))
    if fmt == "e4m3":
        words = by_word.astype(ml_dtypes.float8_e4m3fn).view(np.uint8)
    else:
        c = by_word.astype(ml_dtypes.float4_e2m1fn).view(np.uint8) & 0xF
        words = (c[..., 0::2] | (c[..., 1::2] << 4)).reshape(k // 512, 128, 2 * n)
    return np.ascontiguousarray(words), np.ascontiguousarray(byte.astype(np.uint8).reshape(k // 512, 16, n))


def unpack_weight(words, scales, fmt):
    g, _, n = scales.shape
    words = np.ascontiguousarray(words).reshape(g, 128, n, -1)
    if fmt == "e4m3":
        vals = words.view(ml_dtypes.float8_e4m3fn).astype(np.float64)
    else:
        nib = np.empty((g, 128, n, 4), np.uint8)
        nib[..., 0::2] = words & 0xF
        nib[..., 1::2] = words >> 4
        vals = E2M1[nib]
    vals = vals * np.repeat(np.exp2(scales.astype(np.float64) - 127.0), 8, axis=1)[..., None]
    return vals.transpose(0, 1, 3, 2).reshape(g * 512, n)


def gelu(v):
    return 0.5 * v * (1.0 + np.tanh(np.sqrt(2.0 / np.pi) * (v + 0.044715 * v**3)))


K, H, T, S, T3, S2, T2, P = 1024, 1024, 2048, 512, 2048, 1024, 1024, 512

def setup_inputs():
    n = np.random.standard_normal
    s = mx_kscale(K)[:, None]
    u = mx_kscale(H)[:, None]
    tab_words, tab_scales = pack_weight(n((K, T)) * s, "e4m3")
    w4_words, w4_scales = pack_weight(1.4 * n((K, H)) / np.sqrt(K) / s, "e2m1")
    tab2_words, tab2_scales = pack_weight(n((H, T3)) / np.sqrt(H) / u, "e4m3")
    return {
        "tab_words": tab_words, "tab_scales": tab_scales,
        "offs": striped(np.random.permutation(T)[:S]),
        "w1": (0.9 * n((K, H)) / np.sqrt(K) / s * u.T).astype(np.float32),
        "w4_words": w4_words, "w4_scales": w4_scales,
        "gain": (1.2 * np.exp(0.3 * n(H)) * u[:, 0]).astype(np.float32),
        "page0": (n((H, T2)) * u).astype(np.float32),
        "wgs": np.exp(0.3 * n((128, S))).astype(np.float32),
        "offs3": striped(np.random.permutation(T2)[:S]),
        "terrain": (0.6 + 0.8 * n((H, T2))).astype(np.float32),
        "tab2_words": tab2_words, "tab2_scales": tab2_scales,
        "offs2": striped(np.random.permutation(T3)[:S2]),
        "pos1": striped(np.random.permutation(T2)[:P]),
        "pos2": striped(np.random.permutation(T2)[:P]),
        "corridor": n(S2).astype(np.float32),
    }

def reference(tab_words, tab_scales, offs, w1, w4_words, w4_scales, gain, page0, wgs, offs3, terrain,
              tab2_words, tab2_scales, offs2, pos1, pos2, corridor):
    v = unpack_weight(tab_words, tab_scales, "e4m3")[:, unstriped(offs)]
    w4 = unpack_weight(w4_words, w4_scales, "e2m1")
    direct = mxq(f64(w1), 0, "e4m3").T @ v
    bent = np.tanh(w4.T @ v)
    h = direct + f64(gain)[:, None] * bent
    page = f64(page0).copy()
    page[:, unstriped(offs3)] = np.tile(f64(wgs), (H // 128, 1)) * h
    x = mxq(page * f64(terrain), 0, "e4m3")
    v2 = unpack_weight(tab2_words, tab2_scales, "e4m3")[:, unstriped(offs2)]
    e = v2.T @ x
    head = e[:, unstriped(pos1)]
    tail = e[:, unstriped(pos2)]
    return np.maximum(head, tail) * head + f64(corridor)[:, None]

@@ -1,0 +1,298 @@
+from contextlib import ExitStack
+
+import concourse.mybir as mybir
+
+K, H, T, S, T3, S2, T2, PAIRS = 1024, 1024, 2048, 512, 2048, 1024, 1024, 512
+FLOPS = 2 * (2 * K * H * S + H * S2 * T2)
+
+F32 = mybir.dt.float32
+BF16 = mybir.dt.bfloat16
+I32 = mybir.dt.int32
+U32 = mybir.dt.uint32
+U16 = mybir.dt.uint16
+U8 = mybir.dt.uint8
+FP8X4 = mybir.dt.float8_e4m3fn_x4
+FP4X4 = mybir.dt.float4_e2m1fn_x4
+ALU = mybir.AluOpType
+ACT = mybir.ActivationFunctionType
+
+P = 128
+PACK = 4
+PASS = P * PACK
+PASSES = 2
+QUADS = 4
+BANK = 512
+HALVES = T2 // BANK
+SLICES = H // P
+TILES = S2 // P
+
+
+def tile_list_yarding_corridor_scores_kernel(
+    tc, tab_words, tab_scales, offs, w1, w4_words, w4_scales, gain, page0, wgs, offs3, terrain,
+    tab2_words, tab2_scales, offs2, pos1, pos2, corridor, out,
+):
+    nc = tc.nc
+    with ExitStack() as ctx:
+        lists = ctx.enter_context(tc.tile_pool(name="lists", bufs=1))
+        keep = ctx.enter_context(tc.tile_pool(name="keep", bufs=1))
+        ring = ctx.enter_context(tc.tile_pool(name="ring", bufs=2))
+        psum = ctx.enter_context(tc.psum_pool(name="psum", bufs=2))
+
+        def load_list(src, name):
+            tile = lists.tile(list(src.shape), U16, name=name)
+            nc.sync.dma_start(tile[:], src)
+            return tile
+
+        def load_words(src, a, name):
+            tile = keep.tile([P, src.shape[2]], I32, name=name)
+            nc.sync.dma_start(tile[:], src[a].rearrange("p t i -> p (t i)").bitcast(I32))
+            return tile
+
+        def zeroed_bytes(width, name):
+            tile = keep.tile([P, width // 4], I32, name=name)
+            nc.vector.memset(tile[:], 0)
+            return tile
+
+        def load_scales_side_by_side(tile, src):
+            for q in range(QUADS):
+                nc.sync.dma_start(
+                    tile[32 * q : 32 * q + 4, :].rearrange("r (a w) -> r a w", a=PASSES),
+                    src[:, 4 * q : 4 * q + 4, :].bitcast(I32).rearrange("a r w -> r a w"),
+                )
+
+        def load_w1(a, b):
+            raw = ring.tile([P, PACK, PASS], F32, name="w1_raw")
+            rows = w1[a * PASS : (a + 1) * PASS, b * PASS : (b + 1) * PASS]
+            nc.sync.dma_start(raw[:], rows.rearrange("(p j) c -> p j c", j=PACK))
+            return raw
+
+        def quantise(woven, name):
+            codes = keep.tile([P, PASS], U32, name=name + "_codes", align_bytes=64)
+            plane = keep.tile([P, PASS], U8, name=name + "_plane", align_bytes=64)
+            nc.vector.quantize_mx(out=codes[:].bitcast(FP8X4), scales=plane[:], in_=woven[:])
+            return codes, plane
+
+        def weave_w1(raw):
+            woven = ring.tile([P, PACK * PASS], BF16, name="woven", align_bytes=64)
+            nc.scalar.copy(
+                woven[:].rearrange("p (t m j) -> p m j t", t=PACK, j=PACK),
+                raw[:].rearrange("p j (m t) -> p m j t", t=PACK),
+            )
+            return woven
+
+        page_rows = page0.rearrange("(b p t) n -> b t p n", p=P, t=PACK)
+        terrain_rows = terrain.rearrange("(b p t) n -> b t p n", p=P, t=PACK)
+
+        def load_page(s):
+            tile = keep.tile([P, T2], F32, name="page%d" % s)
+            nc.sync.dma_start(tile[:], page_rows[s // PACK, s % PACK])
+            return tile
+
+        def load_terrain(s):
+            tile = ring.tile([P, T2], F32, name="rows", bufs=SLICES)
+            nc.sync.dma_start(tile[:], terrain_rows[s // PACK, s % PACK])
+            return tile
+
+        w4s_raw = zeroed_bytes(PASSES * H, "w4s_raw")
+        tabs_raw = zeroed_bytes(PASSES * T, "tabs_raw")
+        tab2s_raw = zeroed_bytes(T3, "tab2s_raw")
+
+        w4_raw = keep.tile([P, PASSES, 2 * H // 4], I32)
+        nc.sync.dma_start(w4_raw[:], w4_words.bitcast(I32).rearrange("a p w -> p a w"))
+        w1_raw = {(0, 0): load_w1(0, 0)}
+        load_scales_side_by_side(w4s_raw, w4_scales)
+        offs_sb = load_list(offs, "offs_sb")
+        w1_raw[1, 0] = load_w1(1, 0)
+        load_scales_side_by_side(tabs_raw, tab_scales)
+        tab_sb = [load_words(tab_words, a, "tab%d" % a) for a in range(PASSES)]
+        gain_sb = keep.tile([P, PASSES, PACK], F32)
+        nc.sync.dma_start(gain_sb[:], gain.rearrange("(b p t) -> p b t", p=P, t=PACK))
+        offs3_sb = load_list(offs3, "offs3_sb")
+        wgs_rows = wgs.rearrange("(q t) s -> q t s", t=PACK)
+        wgs_first = keep.tile([P, S], F32)
+        wgs_rest = keep.tile([P, PACK - 1, S], F32)
+        for q in range(QUADS):
+            nc.sync.dma_start(wgs_first[32 * q : 32 * q + 32, :], wgs_rows[:, 0, :])
+        page = [load_page(0)]
+        for q in range(QUADS):
+            nc.sync.dma_start(wgs_rest[32 * q : 32 * q + 32, :, :], wgs_rows[:, 1:PACK, :])
+        page.append(load_page(1))
+        terr = [load_terrain(0)]
+        w1_raw[0, 1] = load_w1(0, 1)
+        page.append(load_page(2))
+        terr.append(load_terrain(1))
+        w1_raw[1, 1] = load_w1(1, 1)
+        for s in range(3, SLICES):
+            page.append(load_page(s))
+            terr.append(load_terrain(s - 1))
+        terr.append(load_terrain(SLICES - 1))
+        offs2_sb = load_list(offs2, "offs2_sb")
+        pos1_sb = load_list(pos1, "pos1_sb")
+        pos2_sb = load_list(pos2, "pos2_sb")
+        corridor_sb = keep.tile([P, TILES], F32)
+        with nc.allow_non_contiguous_dma(reason="one offset a partition and tile"):
+            nc.sync.dma_start(corridor_sb[:], corridor.rearrange("(i p) -> p i", p=P))
+        for q in range(QUADS):
+            nc.sync.dma_start(tab2s_raw[32 * q : 32 * q + 8, :], tab2_scales[:, 4 * q : 4 * q + 4, :].bitcast(I32))
+        tab2_sb = [load_words(tab2_words, a, "tab2_%d" % a) for a in range(PASSES)]
+
+        w4_dealt = keep.tile([P, PASSES * H], U16, align_bytes=64)
+        nc.vector.tensor_copy(
+            w4_dealt[:].rearrange("p (g t m) -> p g t m", t=PACK, m=P),
+            w4_raw[:].rearrange("p a w -> p (a w)").bitcast(U16).rearrange("p (g m t) -> p g t m", t=PACK, m=P),
+        )
+        w4s_dealt = keep.tile([P, PASSES * H], U8, align_bytes=64)
+        nc.vector.tensor_copy(
+            w4s_dealt[:].rearrange("p (g t m) -> p g t m", t=PACK, m=P),
+            w4s_raw[:].bitcast(U8).rearrange("p (g m t) -> p g t m", t=PACK, m=P),
+        )
+
+        w1q = {}
+        v_plane = []
+        for a in range(PASSES):
+            plane = keep.tile([P, S], U8, name="v_plane%d" % a, align_bytes=64)
+            nc.vector.tensor_copy(plane[:], tabs_raw[:].bitcast(U8)[:, a * T : (a + 1) * T].indirect(offs_sb[:]))
+            v_plane.append(plane)
+        v_codes = []
+        for a in range(PASSES):
+            w1q[a, 0] = quantise(weave_w1(w1_raw[a, 0]), "w1q%d0" % a)
+            codes = keep.tile([P, S], U32, name="v_codes%d" % a, align_bytes=64)
+            nc.vector.tensor_copy(codes[:], tab_sb[a][:].bitcast(U32).indirect(offs_sb[:]))
+            v_codes.append(codes)
+
+        def features(s):
+            b, t = divmod(s, PACK)
+            direct = psum.tile([P, S], F32, name="direct")
+            bent = psum.tile([P, S], F32, name="bent")
+            for a in range(PASSES):
+                col = a * H + s * P
+                nc.tensor.matmul_mx(
+                    out=bent[:],
+                    lhsT=w4_dealt[:, col : col + P].bitcast(FP4X4),
+                    lhsT_scale=w4s_dealt[:, col : col + P],
+                    rhs=v_codes[a][:].bitcast(FP8X4),
+                    rhs_scale=v_plane[a][:],
+                    start=(a == 0),
+                    stop=(a == PASSES - 1),
+                )
+            for a in range(PASSES):
+                codes, plane = w1q[a, b]
+                nc.tensor.matmul_mx(
+                    out=direct[:],
+                    lhsT=codes[:, t * P : (t + 1) * P].bitcast(FP8X4),
+                    lhsT_scale=plane[:, t * P : (t + 1) * P],
+                    rhs=v_codes[a][:].bitcast(FP8X4),
+                    rhs_scale=v_plane[a][:],
+                    start=(a == 0),
+                    stop=(a == PASSES - 1),
+                )
+            curve = ring.tile([P, S], F32, name="curve")
+            nc.scalar.activation(curve[:], bent[:], ACT.Tanh)
+            h = ring.tile([P, S], F32, name="h")
+            nc.vector.scalar_tensor_tensor(h[:], curve[:], gain_sb[:, b, t : t + 1], direct[:], ALU.mult, ALU.add)
+            return h
+
+        def place(s, h):
+            t = s % PACK
+            weight = wgs_first[:] if t == 0 else wgs_rest[:, t - 1, :]
+            nc.vector.tensor_tensor(page[s][:].indirect(offs3_sb[:]), h[:], weight, ALU.mult)
+
+        prod = {}
+
+        def times_terrain(s):
+            b, t = divmod(s, PACK)
+            if t == 0:
+                prod[b] = ring.tile([P, PACK, T2], BF16, name="prod")
+            width = BANK if t == PACK - 1 else T2
+            for start in range(0, T2, width):
+                cols = slice(start, start + width)
+                nc.vector.tensor_tensor(prod[b][:, t, cols], page[s][:, cols], terr[s][:, cols], ALU.mult)
+
+        def weave_x(b, n):
+            woven = ring.tile([P, PACK * BANK], BF16, name="woven", align_bytes=64)
+            nc.scalar.copy(
+                woven[:].rearrange("p (c i t) -> p c t i", i=4, t=PACK),
+                prod[b][:, :, n * BANK : (n + 1) * BANK].rearrange("p t (c i) -> p c t i", i=4),
+            )
+            return woven
+
+        xq = {}
+        hs = {0: features(0)}
+        for s in range(SLICES):
+            if s == 1:
+                for a in range(PASSES):
+                    w1q[a, 1] = quantise(weave_w1(w1_raw[a, 1]), "w1q%d1" % a)
+            if s + 1 < SLICES:
+                hs[s + 1] = features(s + 1)
+            if s >= 1:
+                times_terrain(s - 1)
+            place(s, hs[s])
+            if s == PACK + 1:
+                for n in range(HALVES):
+                    xq[0, n] = quantise(weave_x(0, n), "xq0%d" % n)
+
+        v2_codes = [keep.tile([P, S2], U32, name="v2_codes%d" % a, align_bytes=64) for a in range(PASSES)]
+        v2_planes = keep.tile([P, S2], U8, align_bytes=64)
+
+        def gather_v2(half):
+            cols = slice(half * BANK, (half + 1) * BANK)
+            entries = offs2_sb[:, half * (BANK // 16) : (half + 1) * (BANK // 16)]
+            nc.vector.tensor_copy(v2_planes[:, cols], tab2s_raw[:].bitcast(U8).indirect(entries))
+            for a in range(PASSES):
+                nc.vector.tensor_copy(v2_codes[a][:, cols], tab2_sb[a][:].bitcast(U32).indirect(entries))
+
+        times_terrain(SLICES - 1)
+        woven_x = [weave_x(1, n) for n in range(HALVES)]
+        gather_v2(0)
+        for n in range(HALVES):
+            xq[1, n] = quantise(woven_x[n], "xq1%d" % n)
+        gather_v2(1)
+
+        def scores(i):
+            e = ring.tile([P, T2], F32, name="rows", bufs=SLICES)
+            cols = slice(i * P, (i + 1) * P)
+            for n in range(HALVES):
+                bank = psum.tile([P, BANK], F32, name="score_bank", bufs=4)
+                for a in range(PASSES):
+                    codes, plane = xq[a, n]
+                    nc.tensor.matmul_mx(
+                        out=bank[:],
+                        lhsT=v2_codes[a][:, cols].bitcast(FP8X4),
+                        lhsT_scale=v2_planes[4 * a : P, cols],
+                        rhs=codes[:].bitcast(FP8X4),
+                        rhs_scale=plane[:],
+                        start=(a == 0),
+                        stop=(a == PASSES - 1),
+                    )
+                nc.scalar.copy(e[:, n * BANK : (n + 1) * BANK], bank[:])
+            return e
+
+        def pick(e):
+            head = ring.tile([P, PAIRS], F32, name="head", bufs=3)
+            tail = ring.tile([P, PAIRS], F32, name="tail")
+            nc.vector.tensor_copy(head[:], e[:].indirect(pos1_sb[:]))
+            nc.vector.tensor_copy(tail[:], e[:].indirect(pos2_sb[:]))
+            return head, tail
+
+        def greater(head, tail):
+            top = ring.tile([P, PAIRS], F32, name="top")
+            nc.vector.tensor_tensor(top[:], head[:], tail[:], ALU.max)
+            return top
+
+        def finish(i, head, top):
+            product = ring.tile([P, PAIRS], F32, name="product")
+            nc.vector.tensor_tensor(product[:], top[:], head[:], ALU.mult)
+            result = ring.tile([P, PAIRS], F32, name="result")
+            nc.scalar.activation(result[:], product[:], ACT.Identity, bias=corridor_sb[:, i : i + 1])
+            nc.sync.dma_start(out[i * P : (i + 1) * P, :], result[:])
+
+        es = {0: scores(0)}
+        pending = None
+        for i in range(TILES):
+            if i + 1 < TILES:
+                es[i + 1] = scores(i + 1)
+            head, tail = pick(es[i])
+            if pending is not None:
+                finish(*pending)
+            pending = (i, head, greater(head, tail))
+        finish(*pending)

@@ -48,9 +48,9 @@ def tile_list_yarding_corridor_scores_kernel(
             nc.sync.dma_start(tile[:], src[a].rearrange("p t i -> p (t i)").bitcast(I32))
             return tile
 
-        def zeroed_bytes(width, name):
+        def zeroed_bytes(engine, width, name):
             tile = keep.tile([P, width // 4], I32, name=name)
-            nc.vector.memset(tile[:], 0)
+            engine.memset(tile[:], 0)
             return tile
 
         def load_scales_side_by_side(tile, src):
@@ -93,21 +93,24 @@ def tile_list_yarding_corridor_scores_kernel(
             nc.sync.dma_start(tile[:], terrain_rows[s // PACK, s % PACK])
             return tile
 
-        w4s_raw = zeroed_bytes(PASSES * H, "w4s_raw")
-        tabs_raw = zeroed_bytes(PASSES * T, "tabs_raw")
-        tab2s_raw = zeroed_bytes(T3, "tab2s_raw")
+        tabs_raw = zeroed_bytes(nc.vector, PASSES * T, "tabs_raw")
+        w4s_raw = zeroed_bytes(nc.gpsimd, PASSES * H, "w4s_raw")
+        tab2s_raw = zeroed_bytes(nc.gpsimd, T3, "tab2s_raw")
 
-        w4_raw = keep.tile([P, PASSES, 2 * H // 4], I32)
-        nc.sync.dma_start(w4_raw[:], w4_words.bitcast(I32).rearrange("a p w -> p a w"))
-        w1_raw = {(0, 0): load_w1(0, 0)}
-        load_scales_side_by_side(w4s_raw, w4_scales)
         offs_sb = load_list(offs, "offs_sb")
-        w1_raw[1, 0] = load_w1(1, 0)
-        load_scales_side_by_side(tabs_raw, tab_scales)
-        tab_sb = [load_words(tab_words, a, "tab%d" % a) for a in range(PASSES)]
+        offs3_sb = load_list(offs3, "offs3_sb")
         gain_sb = keep.tile([P, PASSES, PACK], F32)
         nc.sync.dma_start(gain_sb[:], gain.rearrange("(b p t) -> p b t", p=P, t=PACK))
-        offs3_sb = load_list(offs3, "offs3_sb")
+        offs2_sb = load_list(offs2, "offs2_sb")
+        pos1_sb = load_list(pos1, "pos1_sb")
+        pos2_sb = load_list(pos2, "pos2_sb")
+        w1_raw = {(0, 0): load_w1(0, 0)}
+        w4_raw = keep.tile([P, PASSES, 2 * H // 4], I32)
+        nc.sync.dma_start(w4_raw[:], w4_words.bitcast(I32).rearrange("a p w -> p a w"))
+        load_scales_side_by_side(tabs_raw, tab_scales)
+        w1_raw[1, 0] = load_w1(1, 0)
+        load_scales_side_by_side(w4s_raw, w4_scales)
+        tab_sb = [load_words(tab_words, a, "tab%d" % a) for a in range(PASSES)]
         wgs_rows = wgs.rearrange("(q t) s -> q t s", t=PACK)
         wgs_first = keep.tile([P, S], F32)
         wgs_rest = keep.tile([P, PACK - 1, S], F32)
@@ -126,15 +129,12 @@ def tile_list_yarding_corridor_scores_kernel(
             page.append(load_page(s))
             terr.append(load_terrain(s - 1))
         terr.append(load_terrain(SLICES - 1))
-        offs2_sb = load_list(offs2, "offs2_sb")
-        pos1_sb = load_list(pos1, "pos1_sb")
-        pos2_sb = load_list(pos2, "pos2_sb")
-        corridor_sb = keep.tile([P, TILES], F32)
-        with nc.allow_non_contiguous_dma(reason="one offset a partition and tile"):
-            nc.sync.dma_start(corridor_sb[:], corridor.rearrange("(i p) -> p i", p=P))
         for q in range(QUADS):
             nc.sync.dma_start(tab2s_raw[32 * q : 32 * q + 8, :], tab2_scales[:, 4 * q : 4 * q + 4, :].bitcast(I32))
         tab2_sb = [load_words(tab2_words, a, "tab2_%d" % a) for a in range(PASSES)]
+        corridor_sb = keep.tile([P, TILES], F32)
+        with nc.allow_non_contiguous_dma(reason="one offset a partition and tile"):
+            nc.sync.dma_start(corridor_sb[:], corridor.rearrange("(i p) -> p i", p=P))
 
         w4_dealt = keep.tile([P, PASSES * H], U16, align_bytes=64)
         nc.vector.tensor_copy(
@@ -190,12 +190,14 @@ def tile_list_yarding_corridor_scores_kernel(
             nc.scalar.activation(curve[:], bent[:], ACT.Tanh)
             h = ring.tile([P, S], F32, name="h")
             nc.vector.scalar_tensor_tensor(h[:], curve[:], gain_sb[:, b, t : t + 1], direct[:], ALU.mult, ALU.add)
-            return h
-
-        def place(s, h):
-            t = s % PACK
             weight = wgs_first[:] if t == 0 else wgs_rest[:, t - 1, :]
-            nc.vector.tensor_tensor(page[s][:].indirect(offs3_sb[:]), h[:], weight, ALU.mult)
+            weighted = ring.tile([P, S], F32, name="weighted")
+            engine = nc.vector if s == 0 else nc.gpsimd
+            engine.tensor_tensor(weighted[:], h[:], weight, ALU.mult)
+            return weighted
+
+        def place(s, weighted):
+            nc.vector.tensor_copy(page[s][:].indirect(offs3_sb[:]), weighted[:])
 
         prod = {}
 
@@ -206,7 +208,7 @@ def tile_list_yarding_corridor_scores_kernel(
             width = BANK if t == PACK - 1 else T2
             for start in range(0, T2, width):
                 cols = slice(start, start + width)
-                nc.vector.tensor_tensor(prod[b][:, t, cols], page[s][:, cols], terr[s][:, cols], ALU.mult)
+                nc.gpsimd.tensor_tensor(prod[b][:, t, cols], page[s][:, cols], terr[s][:, cols], ALU.mult)
 
         def weave_x(b, n):
             woven = ring.tile([P, PACK * BANK], BF16, name="woven", align_bytes=64)
@@ -281,7 +283,8 @@ def tile_list_yarding_corridor_scores_kernel(
 
         def finish(i, head, top):
             product = ring.tile([P, PAIRS], F32, name="product")
-            nc.vector.tensor_tensor(product[:], top[:], head[:], ALU.mult)
+            engine = nc.vector if i == TILES - 1 else nc.gpsimd
+            engine.tensor_tensor(product[:], top[:], head[:], ALU.mult)
             result = ring.tile([P, PAIRS], F32, name="result")
             nc.scalar.activation(result[:], product[:], ACT.Identity, bias=corridor_sb[:, i : i + 1])
             nc.sync.dma_start(out[i * P : (i + 1) * P, :], result[:])

@@ -44,7 +44,7 @@ def tile_list_yarding_corridor_scores_kernel(
             return tile
 
         def load_words(src, a, name):
-            tile = keep.tile([P, src.shape[2]], I32, name=name)
+            tile = keep.tile([P, src.shape[2]], I32, name=name, align_bytes=64)
             nc.sync.dma_start(tile[:], src[a].rearrange("p t i -> p (t i)").bitcast(I32))
             return tile
 
@@ -66,8 +66,8 @@ def tile_list_yarding_corridor_scores_kernel(
             nc.sync.dma_start(raw[:], rows.rearrange("(p j) c -> p j c", j=PACK))
             return raw
 
-        def quantise(woven, name):
-            codes = keep.tile([P, PASS], U32, name=name + "_codes", align_bytes=64)
+        def quantise(woven, name, slot=None):
+            codes = keep.tile([P, PASS], U32, name=slot or name + "_codes", align_bytes=64)
             plane = keep.tile([P, PASS], U8, name=name + "_plane", align_bytes=64)
             nc.vector.quantize_mx(out=codes[:].bitcast(FP8X4), scales=plane[:], in_=woven[:])
             return codes, plane
@@ -89,7 +89,10 @@ def tile_list_yarding_corridor_scores_kernel(
             return tile
 
         def load_terrain(s):
-            tile = ring.tile([P, T2], F32, name="rows", bufs=SLICES)
+            if s < SLICES - 2:
+                tile = ring.tile([P, T2], F32, name="rows", bufs=SLICES - 2)
+            else:
+                tile = keep.tile([P, T2], F32, name="late%d" % s, align_bytes=64)
             nc.sync.dma_start(tile[:], terrain_rows[s // PACK, s % PACK])
             return tile
 
@@ -104,9 +107,9 @@ def tile_list_yarding_corridor_scores_kernel(
         offs2_sb = load_list(offs2, "offs2_sb")
         pos1_sb = load_list(pos1, "pos1_sb")
         pos2_sb = load_list(pos2, "pos2_sb")
-        w1_raw = {(0, 0): load_w1(0, 0)}
         w4_raw = keep.tile([P, PASSES, 2 * H // 4], I32)
         nc.sync.dma_start(w4_raw[:], w4_words.bitcast(I32).rearrange("a p w -> p a w"))
+        w1_raw = {(0, 0): load_w1(0, 0)}
         load_scales_side_by_side(tabs_raw, tab_scales)
         w1_raw[1, 0] = load_w1(1, 0)
         load_scales_side_by_side(w4s_raw, w4_scales)
@@ -128,10 +131,13 @@ def tile_list_yarding_corridor_scores_kernel(
         for s in range(3, SLICES):
             page.append(load_page(s))
             terr.append(load_terrain(s - 1))
+            if s == SLICES - 2:
+                for q in range(QUADS):
+                    nc.sync.dma_start(
+                        tab2s_raw[32 * q : 32 * q + 8, :], tab2_scales[:, 4 * q : 4 * q + 4, :].bitcast(I32)
+                    )
+                tab2_sb = [load_words(tab2_words, a, "tab2_%d" % a) for a in range(PASSES)]
         terr.append(load_terrain(SLICES - 1))
-        for q in range(QUADS):
-            nc.sync.dma_start(tab2s_raw[32 * q : 32 * q + 8, :], tab2_scales[:, 4 * q : 4 * q + 4, :].bitcast(I32))
-        tab2_sb = [load_words(tab2_words, a, "tab2_%d" % a) for a in range(PASSES)]
         corridor_sb = keep.tile([P, TILES], F32)
         with nc.allow_non_contiguous_dma(reason="one offset a partition and tile"):
             nc.sync.dma_start(corridor_sb[:], corridor.rearrange("(i p) -> p i", p=P))
@@ -141,24 +147,27 @@ def tile_list_yarding_corridor_scores_kernel(
             w4_dealt[:].rearrange("p (g t m) -> p g t m", t=PACK, m=P),
             w4_raw[:].rearrange("p a w -> p (a w)").bitcast(U16).rearrange("p (g m t) -> p g t m", t=PACK, m=P),
         )
-        w4s_dealt = keep.tile([P, PASSES * H], U8, align_bytes=64)
-        nc.vector.tensor_copy(
-            w4s_dealt[:].rearrange("p (g t m) -> p g t m", t=PACK, m=P),
-            w4s_raw[:].bitcast(U8).rearrange("p (g m t) -> p g t m", t=PACK, m=P),
-        )
-
         w1q = {}
         v_plane = []
         for a in range(PASSES):
             plane = keep.tile([P, S], U8, name="v_plane%d" % a, align_bytes=64)
             nc.vector.tensor_copy(plane[:], tabs_raw[:].bitcast(U8)[:, a * T : (a + 1) * T].indirect(offs_sb[:]))
             v_plane.append(plane)
-        v_codes = []
-        for a in range(PASSES):
-            w1q[a, 0] = quantise(weave_w1(w1_raw[a, 0]), "w1q%d0" % a)
+        w1q[0, 0] = quantise(weave_w1(w1_raw[0, 0]), "w1q00")
+        w4s_dealt = keep.tile([P, PASSES * H], U8, align_bytes=64)
+        nc.vector.tensor_copy(
+            w4s_dealt[:].rearrange("p (g t m) -> p g t m", t=PACK, m=P),
+            w4s_raw[:].bitcast(U8).rearrange("p (g m t) -> p g t m", t=PACK, m=P),
+        )
+
+        def gather_v(a):
             codes = keep.tile([P, S], U32, name="v_codes%d" % a, align_bytes=64)
             nc.vector.tensor_copy(codes[:], tab_sb[a][:].bitcast(U32).indirect(offs_sb[:]))
-            v_codes.append(codes)
+            return codes
+
+        v_codes = [gather_v(0)]
+        w1q[1, 0] = quantise(weave_w1(w1_raw[1, 0]), "w1q10", slot="tab0")
+        v_codes.append(gather_v(1))
 
         def features(s):
             b, t = divmod(s, PACK)
@@ -205,10 +214,11 @@ def tile_list_yarding_corridor_scores_kernel(
             b, t = divmod(s, PACK)
             if t == 0:
                 prod[b] = ring.tile([P, PACK, T2], BF16, name="prod")
-            width = BANK if t == PACK - 1 else T2
+            width = BANK if s == SLICES - 1 else T2
+            engine = nc.vector if s == SLICES - 1 else nc.gpsimd
             for start in range(0, T2, width):
                 cols = slice(start, start + width)
-                nc.gpsimd.tensor_tensor(prod[b][:, t, cols], page[s][:, cols], terr[s][:, cols], ALU.mult)
+                engine.tensor_tensor(prod[b][:, t, cols], page[s][:, cols], terr[s][:, cols], ALU.mult)
 
         def weave_x(b, n):
             woven = ring.tile([P, PACK * BANK], BF16, name="woven", align_bytes=64)
@@ -233,25 +243,26 @@ def tile_list_yarding_corridor_scores_kernel(
                 for n in range(HALVES):
                     xq[0, n] = quantise(weave_x(0, n), "xq0%d" % n)
 
-        v2_codes = [keep.tile([P, S2], U32, name="v2_codes%d" % a, align_bytes=64) for a in range(PASSES)]
-        v2_planes = keep.tile([P, S2], U8, align_bytes=64)
+        def entries2(half):
+            return offs2_sb[:, half * (BANK // 16) : (half + 1) * (BANK // 16)]
 
-        def gather_v2(half):
-            cols = slice(half * BANK, (half + 1) * BANK)
-            entries = offs2_sb[:, half * (BANK // 16) : (half + 1) * (BANK // 16)]
-            nc.vector.tensor_copy(v2_planes[:, cols], tab2s_raw[:].bitcast(U8).indirect(entries))
-            for a in range(PASSES):
-                nc.vector.tensor_copy(v2_codes[a][:, cols], tab2_sb[a][:].bitcast(U32).indirect(entries))
+        def gather_v2(dst, a, half):
+            nc.vector.tensor_copy(dst, tab2_sb[a][:].bitcast(U32).indirect(entries2(half)))
+            return dst
 
         times_terrain(SLICES - 1)
         woven_x = [weave_x(1, n) for n in range(HALVES)]
-        gather_v2(0)
+        v2_first = keep.tile([P, PASSES, BANK], U32, name="late%d" % (SLICES - 2), align_bytes=64)
+        v2_codes = {(a, 0): gather_v2(v2_first[:, a, :], a, 0) for a in range(PASSES)}
+        v2_planes = keep.tile([P, S2], U8, name="late%d" % (SLICES - 1), align_bytes=64)
+        nc.vector.tensor_copy(v2_planes[:], tab2s_raw[:].bitcast(U8).indirect(offs2_sb[:]))
         for n in range(HALVES):
             xq[1, n] = quantise(woven_x[n], "xq1%d" % n)
-        gather_v2(1)
+            later = ring.tile([P, BANK], U32, name="woven", align_bytes=64)
+            v2_codes[n, 1] = gather_v2(later[:], n, 1)
 
         def scores(i):
-            e = ring.tile([P, T2], F32, name="rows", bufs=SLICES)
+            e = ring.tile([P, T2], F32, name="rows", bufs=SLICES - 2)
             cols = slice(i * P, (i + 1) * P)
             for n in range(HALVES):
                 bank = psum.tile([P, BANK], F32, name="score_bank", bufs=4)
@@ -259,7 +270,7 @@ def tile_list_yarding_corridor_scores_kernel(
                     codes, plane = xq[a, n]
                     nc.tensor.matmul_mx(
                         out=bank[:],
-                        lhsT=v2_codes[a][:, cols].bitcast(FP8X4),
+                        lhsT=v2_codes[a, i // PACK][:, (i % PACK) * P : (i % PACK + 1) * P].bitcast(FP8X4),
                         lhsT_scale=v2_planes[4 * a : P, cols],
                         rhs=codes[:].bitcast(FP8X4),
                         rhs_scale=plane[:],
@@ -269,33 +280,34 @@ def tile_list_yarding_corridor_scores_kernel(
                 nc.scalar.copy(e[:, n * BANK : (n + 1) * BANK], bank[:])
             return e
 
-        def pick(e):
-            head = ring.tile([P, PAIRS], F32, name="head", bufs=3)
-            tail = ring.tile([P, PAIRS], F32, name="tail")
-            nc.vector.tensor_copy(head[:], e[:].indirect(pos1_sb[:]))
-            nc.vector.tensor_copy(tail[:], e[:].indirect(pos2_sb[:]))
+        def pick(e, lo, hi):
+            head = ring.tile([P, hi - lo], F32, name="head", bufs=3)
+            tail = ring.tile([P, hi - lo], F32, name="tail")
+            nc.vector.tensor_copy(head[:], e[:].indirect(pos1_sb[:, lo // 16 : hi // 16]))
+            nc.vector.tensor_copy(tail[:], e[:].indirect(pos2_sb[:, lo // 16 : hi // 16]))
             return head, tail
 
         def greater(head, tail):
-            top = ring.tile([P, PAIRS], F32, name="top")
+            top = ring.tile(list(head[:].shape), F32, name="top")
             nc.vector.tensor_tensor(top[:], head[:], tail[:], ALU.max)
             return top
 
-        def finish(i, head, top):
-            product = ring.tile([P, PAIRS], F32, name="product")
-            engine = nc.vector if i == TILES - 1 else nc.gpsimd
-            engine.tensor_tensor(product[:], top[:], head[:], ALU.mult)
-            result = ring.tile([P, PAIRS], F32, name="result")
+        def finish(i, lo, hi, head, top):
+            product = ring.tile([P, hi - lo], F32, name="product")
+            nc.vector.tensor_tensor(product[:], top[:], head[:], ALU.mult)
+            result = ring.tile([P, hi - lo], F32, name="result")
             nc.scalar.activation(result[:], product[:], ACT.Identity, bias=corridor_sb[:, i : i + 1])
-            nc.sync.dma_start(out[i * P : (i + 1) * P, :], result[:])
+            nc.sync.dma_start(out[i * P : (i + 1) * P, lo:hi], result[:])
 
+        pieces = [(i, 0, PAIRS) for i in range(TILES - 1)]
+        pieces = pieces + [(TILES - 1, 0, PAIRS // 2), (TILES - 1, PAIRS // 2, PAIRS)]
         es = {0: scores(0)}
         pending = None
-        for i in range(TILES):
+        for i, lo, hi in pieces:
             if i + 1 < TILES:
                 es[i + 1] = scores(i + 1)
-            head, tail = pick(es[i])
+            head, tail = pick(es[i], lo, hi)
             if pending is not None:
                 finish(*pending)
-            pending = (i, head, greater(head, tail))
+            pending = (i, lo, hi, head, greater(head, tail))
         finish(*pending)

@@ -49,7 +49,7 @@ def tile_list_yarding_corridor_scores_kernel(
             return tile
 
         def zeroed_bytes(engine, width, name):
-            tile = keep.tile([P, width // 4], I32, name=name)
+            tile = keep.tile([P, width // 4], I32, name=name, align_bytes=64)
             engine.memset(tile[:], 0)
             return tile
 
@@ -89,10 +89,10 @@ def tile_list_yarding_corridor_scores_kernel(
             return tile
 
         def load_terrain(s):
-            if s < SLICES - 2:
-                tile = ring.tile([P, T2], F32, name="rows", bufs=SLICES - 2)
+            if s < SLICES - 1:
+                tile = ring.tile([P, T2], F32, name="rows", bufs=SLICES - 1)
             else:
-                tile = keep.tile([P, T2], F32, name="late%d" % s, align_bytes=64)
+                tile = keep.tile([P, T2], F32, name="last_terrain", align_bytes=64)
             nc.sync.dma_start(tile[:], terrain_rows[s // PACK, s % PACK])
             return tile
 
@@ -116,7 +116,7 @@ def tile_list_yarding_corridor_scores_kernel(
         tab_sb = [load_words(tab_words, a, "tab%d" % a) for a in range(PASSES)]
         wgs_rows = wgs.rearrange("(q t) s -> q t s", t=PACK)
         wgs_first = keep.tile([P, S], F32)
-        wgs_rest = keep.tile([P, PACK - 1, S], F32)
+        wgs_rest = keep.tile([P, PACK - 1, S], F32, align_bytes=64)
         for q in range(QUADS):
             nc.sync.dma_start(wgs_first[32 * q : 32 * q + 32, :], wgs_rows[:, 0, :])
         page = [load_page(0)]
@@ -153,60 +153,60 @@ def tile_list_yarding_corridor_scores_kernel(
             plane = keep.tile([P, S], U8, name="v_plane%d" % a, align_bytes=64)
             nc.vector.tensor_copy(plane[:], tabs_raw[:].bitcast(U8)[:, a * T : (a + 1) * T].indirect(offs_sb[:]))
             v_plane.append(plane)
-        w1q[0, 0] = quantise(weave_w1(w1_raw[0, 0]), "w1q00")
+        w1q[0, 0] = quantise(weave_w1(w1_raw[0, 0]), "w1q00", slot="tabs_raw")
         w4s_dealt = keep.tile([P, PASSES * H], U8, align_bytes=64)
         nc.vector.tensor_copy(
             w4s_dealt[:].rearrange("p (g t m) -> p g t m", t=PACK, m=P),
             w4s_raw[:].bitcast(U8).rearrange("p (g m t) -> p g t m", t=PACK, m=P),
         )
 
-        def gather_v(a):
-            codes = keep.tile([P, S], U32, name="v_codes%d" % a, align_bytes=64)
-            nc.vector.tensor_copy(codes[:], tab_sb[a][:].bitcast(U32).indirect(offs_sb[:]))
+        def gather_v(a, slot, width):
+            codes = keep.tile([P, S], U32, name=slot, align_bytes=64)
+            for lo in range(0, S, width):
+                entries = offs_sb[:, lo // 16 : (lo + width) // 16]
+                nc.vector.tensor_copy(codes[:, lo : lo + width], tab_sb[a][:].bitcast(U32).indirect(entries))
             return codes
 
-        v_codes = [gather_v(0)]
+        v_codes = [gather_v(0, "w4s_raw", S)]
         w1q[1, 0] = quantise(weave_w1(w1_raw[1, 0]), "w1q10", slot="tab0")
-        v_codes.append(gather_v(1))
+        v_codes.append(gather_v(1, "v_codes1", S // 2))
 
-        def features(s):
+        def features(s, lo, hi):
             b, t = divmod(s, PACK)
-            direct = psum.tile([P, S], F32, name="direct")
-            bent = psum.tile([P, S], F32, name="bent")
+            direct = psum.tile([P, hi - lo], F32, name="direct")
+            bent = psum.tile([P, hi - lo], F32, name="bent")
             for a in range(PASSES):
                 col = a * H + s * P
+                codes, plane = w1q[a, b]
                 nc.tensor.matmul_mx(
                     out=bent[:],
                     lhsT=w4_dealt[:, col : col + P].bitcast(FP4X4),
                     lhsT_scale=w4s_dealt[:, col : col + P],
-                    rhs=v_codes[a][:].bitcast(FP8X4),
-                    rhs_scale=v_plane[a][:],
+                    rhs=v_codes[a][:, lo:hi].bitcast(FP8X4),
+                    rhs_scale=v_plane[a][:, lo:hi],
                     start=(a == 0),
                     stop=(a == PASSES - 1),
                 )
-            for a in range(PASSES):
-                codes, plane = w1q[a, b]
                 nc.tensor.matmul_mx(
                     out=direct[:],
                     lhsT=codes[:, t * P : (t + 1) * P].bitcast(FP8X4),
                     lhsT_scale=plane[:, t * P : (t + 1) * P],
-                    rhs=v_codes[a][:].bitcast(FP8X4),
-                    rhs_scale=v_plane[a][:],
+                    rhs=v_codes[a][:, lo:hi].bitcast(FP8X4),
+                    rhs_scale=v_plane[a][:, lo:hi],
                     start=(a == 0),
                     stop=(a == PASSES - 1),
                 )
-            curve = ring.tile([P, S], F32, name="curve")
+            curve = ring.tile([P, hi - lo], F32, name="curve")
             nc.scalar.activation(curve[:], bent[:], ACT.Tanh)
-            h = ring.tile([P, S], F32, name="h")
+            h = ring.tile([P, hi - lo], F32, name="h")
             nc.vector.scalar_tensor_tensor(h[:], curve[:], gain_sb[:, b, t : t + 1], direct[:], ALU.mult, ALU.add)
-            weight = wgs_first[:] if t == 0 else wgs_rest[:, t - 1, :]
-            weighted = ring.tile([P, S], F32, name="weighted")
-            engine = nc.vector if s == 0 else nc.gpsimd
-            engine.tensor_tensor(weighted[:], h[:], weight, ALU.mult)
-            return weighted
+            return h
 
-        def place(s, weighted):
-            nc.vector.tensor_copy(page[s][:].indirect(offs3_sb[:]), weighted[:])
+        def place(s, lo, hi, h):
+            t = s % PACK
+            weight = wgs_first[:, lo:hi] if t == 0 else wgs_rest[:, t - 1, lo:hi]
+            window = page[s][:].indirect(offs3_sb[:, lo // 16 : hi // 16])
+            nc.vector.tensor_tensor(window, h[:], weight, ALU.mult)
 
         prod = {}
 
@@ -215,10 +215,9 @@ def tile_list_yarding_corridor_scores_kernel(
             if t == 0:
                 prod[b] = ring.tile([P, PACK, T2], BF16, name="prod")
             width = BANK if s == SLICES - 1 else T2
-            engine = nc.vector if s == SLICES - 1 else nc.gpsimd
             for start in range(0, T2, width):
                 cols = slice(start, start + width)
-                engine.tensor_tensor(prod[b][:, t, cols], page[s][:, cols], terr[s][:, cols], ALU.mult)
+                nc.vector.tensor_tensor(prod[b][:, t, cols], page[s][:, cols], terr[s][:, cols], ALU.mult)
 
         def weave_x(b, n):
             woven = ring.tile([P, PACK * BANK], BF16, name="woven", align_bytes=64)
@@ -229,49 +228,55 @@ def tile_list_yarding_corridor_scores_kernel(
             return woven
 
         xq = {}
-        hs = {0: features(0)}
-        for s in range(SLICES):
+        steps = [(0, 0, S // 2), (0, S // 2, S)] + [(s, 0, S) for s in range(1, SLICES)]
+        h_next = features(*steps[0])
+        for step, (s, lo, hi) in enumerate(steps):
+            h_now = h_next
             if s == 1:
                 for a in range(PASSES):
                     w1q[a, 1] = quantise(weave_w1(w1_raw[a, 1]), "w1q%d1" % a)
-            if s + 1 < SLICES:
-                hs[s + 1] = features(s + 1)
+            if step + 1 < len(steps):
+                h_next = features(*steps[step + 1])
             if s >= 1:
                 times_terrain(s - 1)
-            place(s, hs[s])
+            place(s, lo, hi, h_now)
             if s == PACK + 1:
                 for n in range(HALVES):
                     xq[0, n] = quantise(weave_x(0, n), "xq0%d" % n)
 
-        def entries2(half):
-            return offs2_sb[:, half * (BANK // 16) : (half + 1) * (BANK // 16)]
+        def gather_v2_words(pool, slot, half):
+            codes = pool.tile([P, PASSES, BANK], U32, name=slot, align_bytes=64)
+            entries = offs2_sb[:, half * (BANK // 16) : (half + 1) * (BANK // 16)]
+            for a in range(PASSES):
+                nc.vector.tensor_copy(codes[:, a, :], tab2_sb[a][:].bitcast(U32).indirect(entries))
+            return codes
 
-        def gather_v2(dst, a, half):
-            nc.vector.tensor_copy(dst, tab2_sb[a][:].bitcast(U32).indirect(entries2(half)))
-            return dst
+        def gather_v2_planes(pool, slot, half):
+            planes = pool.tile([P, BANK], U8, name=slot, align_bytes=64)
+            entries = offs2_sb[:, half * (BANK // 16) : (half + 1) * (BANK // 16)]
+            nc.vector.tensor_copy(planes[:], tab2s_raw[:].bitcast(U8).indirect(entries))
+            return planes
 
         times_terrain(SLICES - 1)
         woven_x = [weave_x(1, n) for n in range(HALVES)]
-        v2_first = keep.tile([P, PASSES, BANK], U32, name="late%d" % (SLICES - 2), align_bytes=64)
-        v2_codes = {(a, 0): gather_v2(v2_first[:, a, :], a, 0) for a in range(PASSES)}
-        v2_planes = keep.tile([P, S2], U8, name="late%d" % (SLICES - 1), align_bytes=64)
-        nc.vector.tensor_copy(v2_planes[:], tab2s_raw[:].bitcast(U8).indirect(offs2_sb[:]))
-        for n in range(HALVES):
-            xq[1, n] = quantise(woven_x[n], "xq1%d" % n)
-            later = ring.tile([P, BANK], U32, name="woven", align_bytes=64)
-            v2_codes[n, 1] = gather_v2(later[:], n, 1)
+        v2_codes = [gather_v2_words(keep, "last_terrain", 0)]
+        v2_planes = [gather_v2_planes(keep, "wgs_rest", 0)]
+        xq[1, 0] = quantise(woven_x[0], "xq10")
+        v2_planes.append(gather_v2_planes(ring, "woven", 1))
+        xq[1, 1] = quantise(woven_x[1], "xq11")
+        v2_codes.append(gather_v2_words(ring, "woven", 1))
 
         def scores(i):
-            e = ring.tile([P, T2], F32, name="rows", bufs=SLICES - 2)
-            cols = slice(i * P, (i + 1) * P)
+            e = ring.tile([P, T2], F32, name="rows", bufs=SLICES - 1)
+            half, cols = i // PACK, slice((i % PACK) * P, (i % PACK + 1) * P)
             for n in range(HALVES):
                 bank = psum.tile([P, BANK], F32, name="score_bank", bufs=4)
                 for a in range(PASSES):
                     codes, plane = xq[a, n]
                     nc.tensor.matmul_mx(
                         out=bank[:],
-                        lhsT=v2_codes[a, i // PACK][:, (i % PACK) * P : (i % PACK + 1) * P].bitcast(FP8X4),
-                        lhsT_scale=v2_planes[4 * a : P, cols],
+                        lhsT=v2_codes[half][:, a, cols].bitcast(FP8X4),
+                        lhsT_scale=v2_planes[half][4 * a : P, cols],
                         rhs=codes[:].bitcast(FP8X4),
                         rhs_scale=plane[:],
                         start=(a == 0),
@@ -280,21 +285,17 @@ def tile_list_yarding_corridor_scores_kernel(
                 nc.scalar.copy(e[:, n * BANK : (n + 1) * BANK], bank[:])
             return e
 
-        def pick(e, lo, hi):
-            head = ring.tile([P, hi - lo], F32, name="head", bufs=3)
-            tail = ring.tile([P, hi - lo], F32, name="tail")
-            nc.vector.tensor_copy(head[:], e[:].indirect(pos1_sb[:, lo // 16 : hi // 16]))
-            nc.vector.tensor_copy(tail[:], e[:].indirect(pos2_sb[:, lo // 16 : hi // 16]))
-            return head, tail
+        def pick(e, positions, lo, hi, name):
+            picked = ring.tile([P, hi - lo], F32, name=name, bufs=3)
+            nc.vector.tensor_copy(picked[:], e[:].indirect(positions[:, lo // 16 : hi // 16]))
+            return picked
 
-        def greater(head, tail):
-            top = ring.tile(list(head[:].shape), F32, name="top")
+        def finish(i, lo, hi, head, tail):
+            top = ring.tile([P, hi - lo], F32, name="top")
             nc.vector.tensor_tensor(top[:], head[:], tail[:], ALU.max)
-            return top
-
-        def finish(i, lo, hi, head, top):
             product = ring.tile([P, hi - lo], F32, name="product")
-            nc.vector.tensor_tensor(product[:], top[:], head[:], ALU.mult)
+            engine = nc.vector if i == TILES - 1 else nc.gpsimd
+            engine.tensor_tensor(product[:], top[:], head[:], ALU.mult)
             result = ring.tile([P, hi - lo], F32, name="result")
             nc.scalar.activation(result[:], product[:], ACT.Identity, bias=corridor_sb[:, i : i + 1])
             nc.sync.dma_start(out[i * P : (i + 1) * P, lo:hi], result[:])
@@ -306,8 +307,8 @@ def tile_list_yarding_corridor_scores_kernel(
         for i, lo, hi in pieces:
             if i + 1 < TILES:
                 es[i + 1] = scores(i + 1)
-            head, tail = pick(es[i], lo, hi)
+            head = pick(es[i], pos1_sb, lo, hi, "head")
             if pending is not None:
                 finish(*pending)
-            pending = (i, lo, hi, head, greater(head, tail))
+            pending = (i, lo, hi, head, pick(es[i], pos2_sb, lo, hi, "tail"))
         finish(*pending)

@@ -21,10 +21,13 @@ PACK = 4
 PASS = P * PACK
 PASSES = 2
 QUADS = 4
+QUAD = P // QUADS
+GROUP = 16
 BANK = 512
 HALVES = T2 // BANK
 SLICES = H // P
 TILES = S2 // P
+ALIGN = 64
 
 
 def tile_list_yarding_corridor_scores_kernel(
@@ -43,21 +46,24 @@ def tile_list_yarding_corridor_scores_kernel(
             nc.sync.dma_start(tile[:], src)
             return tile
 
+        def entries(list_tile, lo, hi):
+            return list_tile[:, lo // GROUP : hi // GROUP]
+
         def load_words(src, a, name):
-            tile = keep.tile([P, src.shape[2]], I32, name=name, align_bytes=64)
+            tile = keep.tile([P, src.shape[2]], I32, name=name, align_bytes=ALIGN)
             nc.sync.dma_start(tile[:], src[a].rearrange("p t i -> p (t i)").bitcast(I32))
             return tile
 
         def zeroed_bytes(engine, width, name):
-            tile = keep.tile([P, width // 4], I32, name=name, align_bytes=64)
+            tile = keep.tile([P, width // 4], I32, name=name, align_bytes=ALIGN)
             engine.memset(tile[:], 0)
             return tile
 
-        def load_scales_side_by_side(tile, src):
-            for q in range(QUADS):
+        def load_planes_side_by_side(tile, src):
+            for r in range(PACK):
                 nc.sync.dma_start(
-                    tile[32 * q : 32 * q + 4, :].rearrange("r (a w) -> r a w", a=PASSES),
-                    src[:, 4 * q : 4 * q + 4, :].bitcast(I32).rearrange("a r w -> r a w"),
+                    tile[r:P:QUAD, :].rearrange("q (a w) -> q a w", a=PASSES),
+                    src[:, r : PACK * QUADS : PACK, :].bitcast(I32).rearrange("a q w -> q a w"),
                 )
 
         def load_w1(a, b):
@@ -65,20 +71,6 @@ def tile_list_yarding_corridor_scores_kernel(
             rows = w1[a * PASS : (a + 1) * PASS, b * PASS : (b + 1) * PASS]
             nc.sync.dma_start(raw[:], rows.rearrange("(p j) c -> p j c", j=PACK))
             return raw
-
-        def quantise(woven, name, slot=None):
-            codes = keep.tile([P, PASS], U32, name=slot or name + "_codes", align_bytes=64)
-            plane = keep.tile([P, PASS], U8, name=name + "_plane", align_bytes=64)
-            nc.vector.quantize_mx(out=codes[:].bitcast(FP8X4), scales=plane[:], in_=woven[:])
-            return codes, plane
-
-        def weave_w1(raw):
-            woven = ring.tile([P, PACK * PASS], BF16, name="woven", align_bytes=64)
-            nc.scalar.copy(
-                woven[:].rearrange("p (t m j) -> p m j t", t=PACK, j=PACK),
-                raw[:].rearrange("p j (m t) -> p m j t", t=PACK),
-            )
-            return woven
 
         page_rows = page0.rearrange("(b p t) n -> b t p n", p=P, t=PACK)
         terrain_rows = terrain.rearrange("(b p t) n -> b t p n", p=P, t=PACK)
@@ -88,17 +80,20 @@ def tile_list_yarding_corridor_scores_kernel(
             nc.sync.dma_start(tile[:], page_rows[s // PACK, s % PACK])
             return tile
 
+        def row_tile():
+            return ring.tile([P, T2], F32, name="rows", bufs=SLICES - 1)
+
         def load_terrain(s):
             if s < SLICES - 1:
-                tile = ring.tile([P, T2], F32, name="rows", bufs=SLICES - 1)
+                tile = row_tile()
             else:
-                tile = keep.tile([P, T2], F32, name="last_terrain", align_bytes=64)
+                tile = keep.tile([P, T2], F32, name="last_terrain", align_bytes=ALIGN)
             nc.sync.dma_start(tile[:], terrain_rows[s // PACK, s % PACK])
             return tile
 
-        tabs_raw = zeroed_bytes(nc.vector, PASSES * T, "tabs_raw")
-        w4s_raw = zeroed_bytes(nc.gpsimd, PASSES * H, "w4s_raw")
-        tab2s_raw = zeroed_bytes(nc.gpsimd, T3, "tab2s_raw")
+        tab_planes_raw = zeroed_bytes(nc.vector, PASSES * T, "tab_planes_raw")
+        w4_planes_raw = zeroed_bytes(nc.gpsimd, PASSES * H, "w4_planes_raw")
+        tab2_planes_raw = zeroed_bytes(nc.gpsimd, T3, "tab2_planes_raw")
 
         offs_sb = load_list(offs, "offs_sb")
         offs3_sb = load_list(offs3, "offs3_sb")
@@ -110,18 +105,19 @@ def tile_list_yarding_corridor_scores_kernel(
         w4_raw = keep.tile([P, PASSES, 2 * H // 4], I32)
         nc.sync.dma_start(w4_raw[:], w4_words.bitcast(I32).rearrange("a p w -> p a w"))
         w1_raw = {(0, 0): load_w1(0, 0)}
-        load_scales_side_by_side(tabs_raw, tab_scales)
+        load_planes_side_by_side(tab_planes_raw, tab_scales)
         w1_raw[1, 0] = load_w1(1, 0)
-        load_scales_side_by_side(w4s_raw, w4_scales)
+        load_planes_side_by_side(w4_planes_raw, w4_scales)
         tab_sb = [load_words(tab_words, a, "tab%d" % a) for a in range(PASSES)]
-        wgs_rows = wgs.rearrange("(q t) s -> q t s", t=PACK)
+        wgs_rows = wgs.rearrange("(u t) s -> u t s", t=PACK)
         wgs_first = keep.tile([P, S], F32)
-        wgs_rest = keep.tile([P, PACK - 1, S], F32, align_bytes=64)
-        for q in range(QUADS):
-            nc.sync.dma_start(wgs_first[32 * q : 32 * q + 32, :], wgs_rows[:, 0, :])
+        wgs_rest = keep.tile([P, PACK - 1, S], F32, align_bytes=ALIGN)
+        quad_order = (0, 2, 1, 3)
+        for q in quad_order:
+            nc.sync.dma_start(wgs_first[QUAD * q : QUAD * (q + 1), :], wgs_rows[:, 0, :])
         page = [load_page(0)]
-        for q in range(QUADS):
-            nc.sync.dma_start(wgs_rest[32 * q : 32 * q + 32, :, :], wgs_rows[:, 1:PACK, :])
+        for q in quad_order:
+            nc.sync.dma_start(wgs_rest[QUAD * q : QUAD * (q + 1), :, :], wgs_rows[:, 1:PACK, :])
         page.append(load_page(1))
         terr = [load_terrain(0)]
         w1_raw[0, 1] = load_w1(0, 1)
@@ -134,41 +130,57 @@ def tile_list_yarding_corridor_scores_kernel(
             if s == SLICES - 2:
                 for q in range(QUADS):
                     nc.sync.dma_start(
-                        tab2s_raw[32 * q : 32 * q + 8, :], tab2_scales[:, 4 * q : 4 * q + 4, :].bitcast(I32)
+                        tab2_planes_raw[QUAD * q : QUAD * q + 8, :], tab2_scales[:, 4 * q : 4 * q + 4, :].bitcast(I32)
                     )
                 tab2_sb = [load_words(tab2_words, a, "tab2_%d" % a) for a in range(PASSES)]
         terr.append(load_terrain(SLICES - 1))
         corridor_sb = keep.tile([P, TILES], F32)
-        with nc.allow_non_contiguous_dma(reason="one offset a partition and tile"):
+        with nc.allow_non_contiguous_dma(reason="one value a partition and tile of candidates"):
             nc.sync.dma_start(corridor_sb[:], corridor.rearrange("(i p) -> p i", p=P))
 
-        w4_dealt = keep.tile([P, PASSES * H], U16, align_bytes=64)
+        def quantise(woven, codes_slot, plane_name):
+            codes = keep.tile([P, PASS], U32, name=codes_slot, align_bytes=ALIGN)
+            plane = keep.tile([P, PASS], U8, name=plane_name, align_bytes=ALIGN)
+            nc.vector.quantize_mx(out=codes[:].bitcast(FP8X4), scales=plane[:], in_=woven[:])
+            return codes, plane
+
+        def weave_w1(raw):
+            woven = ring.tile([P, PACK * PASS], BF16, name="woven", align_bytes=ALIGN)
+            nc.scalar.copy(
+                woven[:].rearrange("p (t m j) -> p m j t", t=PACK, j=PACK),
+                raw[:].rearrange("p j (m t) -> p m j t", t=PACK),
+            )
+            return woven
+
+        w4_dealt = keep.tile([P, PASSES * H], U16, align_bytes=ALIGN)
         nc.vector.tensor_copy(
             w4_dealt[:].rearrange("p (g t m) -> p g t m", t=PACK, m=P),
             w4_raw[:].rearrange("p a w -> p (a w)").bitcast(U16).rearrange("p (g m t) -> p g t m", t=PACK, m=P),
         )
-        w1q = {}
+
         v_plane = []
         for a in range(PASSES):
-            plane = keep.tile([P, S], U8, name="v_plane%d" % a, align_bytes=64)
-            nc.vector.tensor_copy(plane[:], tabs_raw[:].bitcast(U8)[:, a * T : (a + 1) * T].indirect(offs_sb[:]))
+            plane = keep.tile([P, S], U8, name="v_plane%d" % a, align_bytes=ALIGN)
+            window = tab_planes_raw[:].bitcast(U8)[:, a * T : (a + 1) * T]
+            nc.vector.tensor_copy(plane[:], window.indirect(offs_sb[:]))
             v_plane.append(plane)
-        w1q[0, 0] = quantise(weave_w1(w1_raw[0, 0]), "w1q00", slot="tabs_raw")
-        w4s_dealt = keep.tile([P, PASSES * H], U8, align_bytes=64)
+
+        w1q = {(0, 0): quantise(weave_w1(w1_raw[0, 0]), "tab_planes_raw", "w1_plane00")}
+        w4_planes_dealt = keep.tile([P, PASSES * H], U8, align_bytes=ALIGN)
         nc.vector.tensor_copy(
-            w4s_dealt[:].rearrange("p (g t m) -> p g t m", t=PACK, m=P),
-            w4s_raw[:].bitcast(U8).rearrange("p (g m t) -> p g t m", t=PACK, m=P),
+            w4_planes_dealt[:].rearrange("p (g t m) -> p g t m", t=PACK, m=P),
+            w4_planes_raw[:].bitcast(U8).rearrange("p (g m t) -> p g t m", t=PACK, m=P),
         )
 
         def gather_v(a, slot, width):
-            codes = keep.tile([P, S], U32, name=slot, align_bytes=64)
+            codes = keep.tile([P, S], U32, name=slot, align_bytes=ALIGN)
             for lo in range(0, S, width):
-                entries = offs_sb[:, lo // 16 : (lo + width) // 16]
-                nc.vector.tensor_copy(codes[:, lo : lo + width], tab_sb[a][:].bitcast(U32).indirect(entries))
+                window = tab_sb[a][:].bitcast(U32)
+                nc.vector.tensor_copy(codes[:, lo : lo + width], window.indirect(entries(offs_sb, lo, lo + width)))
             return codes
 
-        v_codes = [gather_v(0, "w4s_raw", S)]
-        w1q[1, 0] = quantise(weave_w1(w1_raw[1, 0]), "w1q10", slot="tab0")
+        v_codes = [gather_v(0, "w4_planes_raw", S)]
+        w1q[1, 0] = quantise(weave_w1(w1_raw[1, 0]), "tab0", "w1_plane10")
         v_codes.append(gather_v(1, "v_codes1", S // 2))
 
         def features(s, lo, hi):
@@ -181,7 +193,7 @@ def tile_list_yarding_corridor_scores_kernel(
                 nc.tensor.matmul_mx(
                     out=bent[:],
                     lhsT=w4_dealt[:, col : col + P].bitcast(FP4X4),
-                    lhsT_scale=w4s_dealt[:, col : col + P],
+                    lhsT_scale=w4_planes_dealt[:, col : col + P],
                     rhs=v_codes[a][:, lo:hi].bitcast(FP8X4),
                     rhs_scale=v_plane[a][:, lo:hi],
                     start=(a == 0),
@@ -205,25 +217,25 @@ def tile_list_yarding_corridor_scores_kernel(
         def place(s, lo, hi, h):
             t = s % PACK
             weight = wgs_first[:, lo:hi] if t == 0 else wgs_rest[:, t - 1, lo:hi]
-            window = page[s][:].indirect(offs3_sb[:, lo // 16 : hi // 16])
+            window = page[s][:].indirect(entries(offs3_sb, lo, hi))
             nc.vector.tensor_tensor(window, h[:], weight, ALU.mult)
 
-        prod = {}
+        x_rows = {}
 
         def times_terrain(s):
             b, t = divmod(s, PACK)
             if t == 0:
-                prod[b] = ring.tile([P, PACK, T2], BF16, name="prod")
+                x_rows[b] = ring.tile([P, PACK, T2], BF16, name="x_rows")
             width = BANK if s == SLICES - 1 else T2
             for start in range(0, T2, width):
                 cols = slice(start, start + width)
-                nc.vector.tensor_tensor(prod[b][:, t, cols], page[s][:, cols], terr[s][:, cols], ALU.mult)
+                nc.vector.tensor_tensor(x_rows[b][:, t, cols], page[s][:, cols], terr[s][:, cols], ALU.mult)
 
         def weave_x(b, n):
-            woven = ring.tile([P, PACK * BANK], BF16, name="woven", align_bytes=64)
+            woven = ring.tile([P, PACK * BANK], BF16, name="woven", align_bytes=ALIGN)
             nc.scalar.copy(
                 woven[:].rearrange("p (c i t) -> p c t i", i=4, t=PACK),
-                prod[b][:, :, n * BANK : (n + 1) * BANK].rearrange("p t (c i) -> p c t i", i=4),
+                x_rows[b][:, :, n * BANK : (n + 1) * BANK].rearrange("p t (c i) -> p c t i", i=4),
             )
             return woven
 
@@ -234,7 +246,7 @@ def tile_list_yarding_corridor_scores_kernel(
             h_now = h_next
             if s == 1:
                 for a in range(PASSES):
-                    w1q[a, 1] = quantise(weave_w1(w1_raw[a, 1]), "w1q%d1" % a)
+                    w1q[a, 1] = quantise(weave_w1(w1_raw[a, 1]), "w1_codes%d1" % a, "w1_plane%d1" % a)
             if step + 1 < len(steps):
                 h_next = features(*steps[step + 1])
             if s >= 1:
@@ -242,35 +254,36 @@ def tile_list_yarding_corridor_scores_kernel(
             place(s, lo, hi, h_now)
             if s == PACK + 1:
                 for n in range(HALVES):
-                    xq[0, n] = quantise(weave_x(0, n), "xq0%d" % n)
+                    xq[0, n] = quantise(weave_x(0, n), "x_codes0%d" % n, "x_plane0%d" % n)
 
         def gather_v2_words(pool, slot, half):
-            codes = pool.tile([P, PASSES, BANK], U32, name=slot, align_bytes=64)
-            entries = offs2_sb[:, half * (BANK // 16) : (half + 1) * (BANK // 16)]
+            codes = pool.tile([P, PASSES, BANK], U32, name=slot, align_bytes=ALIGN)
+            picked = entries(offs2_sb, half * BANK, (half + 1) * BANK)
             for a in range(PASSES):
-                nc.vector.tensor_copy(codes[:, a, :], tab2_sb[a][:].bitcast(U32).indirect(entries))
+                nc.vector.tensor_copy(codes[:, a, :], tab2_sb[a][:].bitcast(U32).indirect(picked))
             return codes
 
         def gather_v2_planes(pool, slot, half):
-            planes = pool.tile([P, BANK], U8, name=slot, align_bytes=64)
-            entries = offs2_sb[:, half * (BANK // 16) : (half + 1) * (BANK // 16)]
-            nc.vector.tensor_copy(planes[:], tab2s_raw[:].bitcast(U8).indirect(entries))
+            planes = pool.tile([P, BANK], U8, name=slot, align_bytes=ALIGN)
+            picked = entries(offs2_sb, half * BANK, (half + 1) * BANK)
+            nc.vector.tensor_copy(planes[:], tab2_planes_raw[:].bitcast(U8).indirect(picked))
             return planes
 
         times_terrain(SLICES - 1)
         woven_x = [weave_x(1, n) for n in range(HALVES)]
         v2_codes = [gather_v2_words(keep, "last_terrain", 0)]
         v2_planes = [gather_v2_planes(keep, "wgs_rest", 0)]
-        xq[1, 0] = quantise(woven_x[0], "xq10")
+        xq[1, 0] = quantise(woven_x[0], "x_codes10", "x_plane10")
         v2_planes.append(gather_v2_planes(ring, "woven", 1))
-        xq[1, 1] = quantise(woven_x[1], "xq11")
+        xq[1, 1] = quantise(woven_x[1], "x_codes11", "x_plane11")
         v2_codes.append(gather_v2_words(ring, "woven", 1))
 
         def scores(i):
-            e = ring.tile([P, T2], F32, name="rows", bufs=SLICES - 1)
-            half, cols = i // PACK, slice((i % PACK) * P, (i % PACK + 1) * P)
+            e = row_tile()
+            half, place_in_half = divmod(i, BANK // P)
+            cols = slice(place_in_half * P, (place_in_half + 1) * P)
             for n in range(HALVES):
-                bank = psum.tile([P, BANK], F32, name="score_bank", bufs=4)
+                bank = psum.tile([P, BANK], F32, name="score_bank", bufs=2 * HALVES)
                 for a in range(PASSES):
                     codes, plane = xq[a, n]
                     nc.tensor.matmul_mx(
@@ -287,7 +300,7 @@ def tile_list_yarding_corridor_scores_kernel(
 
         def pick(e, positions, lo, hi, name):
             picked = ring.tile([P, hi - lo], F32, name=name, bufs=3)
-            nc.vector.tensor_copy(picked[:], e[:].indirect(positions[:, lo // 16 : hi // 16]))
+            nc.vector.tensor_copy(picked[:], e[:].indirect(entries(positions, lo, hi)))
             return picked
 
         def finish(i, lo, hi, head, tail):
@@ -302,13 +315,13 @@ def tile_list_yarding_corridor_scores_kernel(
 
         pieces = [(i, 0, PAIRS) for i in range(TILES - 1)]
         pieces = pieces + [(TILES - 1, 0, PAIRS // 2), (TILES - 1, PAIRS // 2, PAIRS)]
-        es = {0: scores(0)}
+        e_tiles = {0: scores(0)}
         pending = None
         for i, lo, hi in pieces:
             if i + 1 < TILES:
-                es[i + 1] = scores(i + 1)
-            head = pick(es[i], pos1_sb, lo, hi, "head")
+                e_tiles[i + 1] = scores(i + 1)
+            head = pick(e_tiles[i], pos1_sb, lo, hi, "head")
             if pending is not None:
                 finish(*pending)
-            pending = (i, lo, hi, head, pick(es[i], pos2_sb, lo, hi, "tail"))
+            pending = (i, lo, hi, head, pick(e_tiles[i], pos2_sb, lo, hi, "tail"))
         finish(*pending)

from contextlib import ExitStack

import concourse.mybir as mybir

K, H, T, S, T3, S2, T2, PAIRS = 1024, 1024, 2048, 512, 2048, 1024, 1024, 512
FLOPS = 2 * (2 * K * H * S + H * S2 * T2)

F32 = mybir.dt.float32
BF16 = mybir.dt.bfloat16
I32 = mybir.dt.int32
U32 = mybir.dt.uint32
U16 = mybir.dt.uint16
U8 = mybir.dt.uint8
FP8X4 = mybir.dt.float8_e4m3fn_x4
FP4X4 = mybir.dt.float4_e2m1fn_x4
ALU = mybir.AluOpType
ACT = mybir.ActivationFunctionType

P = 128
PACK = 4
PASS = P * PACK
PASSES = 2
QUADS = 4
QUAD = P // QUADS
GROUP = 16
BANK = 512
HALVES = T2 // BANK
SLICES = H // P
TILES = S2 // P
ALIGN = 64


def tile_list_yarding_corridor_scores_kernel(
    tc, tab_words, tab_scales, offs, w1, w4_words, w4_scales, gain, page0, wgs, offs3, terrain,
    tab2_words, tab2_scales, offs2, pos1, pos2, corridor, out,
):
    nc = tc.nc
    with ExitStack() as ctx:
        lists = ctx.enter_context(tc.tile_pool(name="lists", bufs=1))
        keep = ctx.enter_context(tc.tile_pool(name="keep", bufs=1))
        ring = ctx.enter_context(tc.tile_pool(name="ring", bufs=2))
        psum = ctx.enter_context(tc.psum_pool(name="psum", bufs=2))

        def load_list(src, name):
            tile = lists.tile(list(src.shape), U16, name=name)
            nc.sync.dma_start(tile[:], src)
            return tile

        def entries(list_tile, lo, hi):
            return list_tile[:, lo // GROUP : hi // GROUP]

        def load_words(src, a, name):
            tile = keep.tile([P, src.shape[2]], I32, name=name, align_bytes=ALIGN)
            nc.sync.dma_start(tile[:], src[a].rearrange("p t i -> p (t i)").bitcast(I32))
            return tile

        def zeroed_bytes(engine, width, name):
            tile = keep.tile([P, width // 4], I32, name=name, align_bytes=ALIGN)
            engine.memset(tile[:], 0)
            return tile

        def load_planes_side_by_side(tile, src):
            for r in range(PACK):
                nc.sync.dma_start(
                    tile[r:P:QUAD, :].rearrange("q (a w) -> q a w", a=PASSES),
                    src[:, r : PACK * QUADS : PACK, :].bitcast(I32).rearrange("a q w -> q a w"),
                )

        def load_w1(a, b):
            raw = ring.tile([P, PACK, PASS], F32, name="w1_raw")
            rows = w1[a * PASS : (a + 1) * PASS, b * PASS : (b + 1) * PASS]
            nc.sync.dma_start(raw[:], rows.rearrange("(p j) c -> p j c", j=PACK))
            return raw

        page_rows = page0.rearrange("(b p t) n -> b t p n", p=P, t=PACK)
        terrain_rows = terrain.rearrange("(b p t) n -> b t p n", p=P, t=PACK)

        def load_page(s):
            tile = keep.tile([P, T2], F32, name="page%d" % s)
            nc.sync.dma_start(tile[:], page_rows[s // PACK, s % PACK])
            return tile

        def row_tile():
            return ring.tile([P, T2], F32, name="rows", bufs=SLICES - 1)

        def load_terrain(s):
            if s < SLICES - 1:
                tile = row_tile()
            else:
                tile = keep.tile([P, T2], F32, name="last_terrain", align_bytes=ALIGN)
            nc.sync.dma_start(tile[:], terrain_rows[s // PACK, s % PACK])
            return tile

        tab_planes_raw = zeroed_bytes(nc.vector, PASSES * T, "tab_planes_raw")
        w4_planes_raw = zeroed_bytes(nc.gpsimd, PASSES * H, "w4_planes_raw")
        tab2_planes_raw = zeroed_bytes(nc.gpsimd, T3, "tab2_planes_raw")

        offs_sb = load_list(offs, "offs_sb")
        offs3_sb = load_list(offs3, "offs3_sb")
        gain_sb = keep.tile([P, PASSES, PACK], F32)
        nc.sync.dma_start(gain_sb[:], gain.rearrange("(b p t) -> p b t", p=P, t=PACK))
        offs2_sb = load_list(offs2, "offs2_sb")
        pos1_sb = load_list(pos1, "pos1_sb")
        pos2_sb = load_list(pos2, "pos2_sb")
        w4_raw = keep.tile([P, PASSES, 2 * H // 4], I32)
        nc.sync.dma_start(w4_raw[:], w4_words.bitcast(I32).rearrange("a p w -> p a w"))
        w1_raw = {(0, 0): load_w1(0, 0)}
        load_planes_side_by_side(tab_planes_raw, tab_scales)
        w1_raw[1, 0] = load_w1(1, 0)
        load_planes_side_by_side(w4_planes_raw, w4_scales)
        tab_sb = [load_words(tab_words, a, "tab%d" % a) for a in range(PASSES)]
        wgs_rows = wgs.rearrange("(u t) s -> u t s", t=PACK)
        wgs_first = keep.tile([P, S], F32)
        wgs_rest = keep.tile([P, PACK - 1, S], F32, align_bytes=ALIGN)
        quad_order = (0, 2, 1, 3)
        for q in quad_order:
            nc.sync.dma_start(wgs_first[QUAD * q : QUAD * (q + 1), :], wgs_rows[:, 0, :])
        page = [load_page(0)]
        for q in quad_order:
            nc.sync.dma_start(wgs_rest[QUAD * q : QUAD * (q + 1), :, :], wgs_rows[:, 1:PACK, :])
        page.append(load_page(1))
        terr = [load_terrain(0)]
        w1_raw[0, 1] = load_w1(0, 1)
        page.append(load_page(2))
        terr.append(load_terrain(1))
        w1_raw[1, 1] = load_w1(1, 1)
        for s in range(3, SLICES):
            page.append(load_page(s))
            terr.append(load_terrain(s - 1))
            if s == SLICES - 2:
                for q in range(QUADS):
                    nc.sync.dma_start(
                        tab2_planes_raw[QUAD * q : QUAD * q + 8, :], tab2_scales[:, 4 * q : 4 * q + 4, :].bitcast(I32)
                    )
                tab2_sb = [load_words(tab2_words, a, "tab2_%d" % a) for a in range(PASSES)]
        terr.append(load_terrain(SLICES - 1))
        corridor_sb = keep.tile([P, TILES], F32)
        with nc.allow_non_contiguous_dma(reason="one value a partition and tile of candidates"):
            nc.sync.dma_start(corridor_sb[:], corridor.rearrange("(i p) -> p i", p=P))

        def quantise(woven, codes_slot, plane_name):
            codes = keep.tile([P, PASS], U32, name=codes_slot, align_bytes=ALIGN)
            plane = keep.tile([P, PASS], U8, name=plane_name, align_bytes=ALIGN)
            nc.vector.quantize_mx(out=codes[:].bitcast(FP8X4), scales=plane[:], in_=woven[:])
            return codes, plane

        def weave_w1(raw):
            woven = ring.tile([P, PACK * PASS], BF16, name="woven", align_bytes=ALIGN)
            nc.scalar.copy(
                woven[:].rearrange("p (t m j) -> p m j t", t=PACK, j=PACK),
                raw[:].rearrange("p j (m t) -> p m j t", t=PACK),
            )
            return woven

        w4_dealt = keep.tile([P, PASSES * H], U16, align_bytes=ALIGN)
        nc.vector.tensor_copy(
            w4_dealt[:].rearrange("p (g t m) -> p g t m", t=PACK, m=P),
            w4_raw[:].rearrange("p a w -> p (a w)").bitcast(U16).rearrange("p (g m t) -> p g t m", t=PACK, m=P),
        )

        v_plane = []
        for a in range(PASSES):
            plane = keep.tile([P, S], U8, name="v_plane%d" % a, align_bytes=ALIGN)
            window = tab_planes_raw[:].bitcast(U8)[:, a * T : (a + 1) * T]
            nc.vector.tensor_copy(plane[:], window.indirect(offs_sb[:]))
            v_plane.append(plane)

        w1q = {(0, 0): quantise(weave_w1(w1_raw[0, 0]), "tab_planes_raw", "w1_plane00")}
        w4_planes_dealt = keep.tile([P, PASSES * H], U8, align_bytes=ALIGN)
        nc.vector.tensor_copy(
            w4_planes_dealt[:].rearrange("p (g t m) -> p g t m", t=PACK, m=P),
            w4_planes_raw[:].bitcast(U8).rearrange("p (g m t) -> p g t m", t=PACK, m=P),
        )

        def gather_v(a, slot, width):
            codes = keep.tile([P, S], U32, name=slot, align_bytes=ALIGN)
            for lo in range(0, S, width):
                window = tab_sb[a][:].bitcast(U32)
                nc.vector.tensor_copy(codes[:, lo : lo + width], window.indirect(entries(offs_sb, lo, lo + width)))
            return codes

        v_codes = [gather_v(0, "w4_planes_raw", S)]
        w1q[1, 0] = quantise(weave_w1(w1_raw[1, 0]), "tab0", "w1_plane10")
        v_codes.append(gather_v(1, "v_codes1", S // 2))

        def features(s, lo, hi):
            b, t = divmod(s, PACK)
            direct = psum.tile([P, hi - lo], F32, name="direct")
            bent = psum.tile([P, hi - lo], F32, name="bent")
            for a in range(PASSES):
                col = a * H + s * P
                codes, plane = w1q[a, b]
                nc.tensor.matmul_mx(
                    out=bent[:],
                    lhsT=w4_dealt[:, col : col + P].bitcast(FP4X4),
                    lhsT_scale=w4_planes_dealt[:, col : col + P],
                    rhs=v_codes[a][:, lo:hi].bitcast(FP8X4),
                    rhs_scale=v_plane[a][:, lo:hi],
                    start=(a == 0),
                    stop=(a == PASSES - 1),
                )
                nc.tensor.matmul_mx(
                    out=direct[:],
                    lhsT=codes[:, t * P : (t + 1) * P].bitcast(FP8X4),
                    lhsT_scale=plane[:, t * P : (t + 1) * P],
                    rhs=v_codes[a][:, lo:hi].bitcast(FP8X4),
                    rhs_scale=v_plane[a][:, lo:hi],
                    start=(a == 0),
                    stop=(a == PASSES - 1),
                )
            curve = ring.tile([P, hi - lo], F32, name="curve")
            nc.scalar.activation(curve[:], bent[:], ACT.Tanh)
            h = ring.tile([P, hi - lo], F32, name="h")
            nc.vector.scalar_tensor_tensor(h[:], curve[:], gain_sb[:, b, t : t + 1], direct[:], ALU.mult, ALU.add)
            return h

        def place(s, lo, hi, h):
            t = s % PACK
            weight = wgs_first[:, lo:hi] if t == 0 else wgs_rest[:, t - 1, lo:hi]
            window = page[s][:].indirect(entries(offs3_sb, lo, hi))
            nc.vector.tensor_tensor(window, h[:], weight, ALU.mult)

        x_rows = {}

        def times_terrain(s):
            b, t = divmod(s, PACK)
            if t == 0:
                x_rows[b] = ring.tile([P, PACK, T2], BF16, name="x_rows")
            width = BANK if s == SLICES - 1 else T2
            for start in range(0, T2, width):
                cols = slice(start, start + width)
                nc.vector.tensor_tensor(x_rows[b][:, t, cols], page[s][:, cols], terr[s][:, cols], ALU.mult)

        def weave_x(b, n):
            woven = ring.tile([P, PACK * BANK], BF16, name="woven", align_bytes=ALIGN)
            nc.scalar.copy(
                woven[:].rearrange("p (c i t) -> p c t i", i=4, t=PACK),
                x_rows[b][:, :, n * BANK : (n + 1) * BANK].rearrange("p t (c i) -> p c t i", i=4),
            )
            return woven

        xq = {}
        steps = [(0, 0, S // 2), (0, S // 2, S)] + [(s, 0, S) for s in range(1, SLICES)]
        h_next = features(*steps[0])
        for step, (s, lo, hi) in enumerate(steps):
            h_now = h_next
            if s == 1:
                for a in range(PASSES):
                    w1q[a, 1] = quantise(weave_w1(w1_raw[a, 1]), "w1_codes%d1" % a, "w1_plane%d1" % a)
            if step + 1 < len(steps):
                h_next = features(*steps[step + 1])
            if s >= 1:
                times_terrain(s - 1)
            place(s, lo, hi, h_now)
            if s == PACK + 1:
                for n in range(HALVES):
                    xq[0, n] = quantise(weave_x(0, n), "x_codes0%d" % n, "x_plane0%d" % n)

        def gather_v2_words(pool, slot, half):
            codes = pool.tile([P, PASSES, BANK], U32, name=slot, align_bytes=ALIGN)
            picked = entries(offs2_sb, half * BANK, (half + 1) * BANK)
            for a in range(PASSES):
                nc.vector.tensor_copy(codes[:, a, :], tab2_sb[a][:].bitcast(U32).indirect(picked))
            return codes

        def gather_v2_planes(pool, slot, half):
            planes = pool.tile([P, BANK], U8, name=slot, align_bytes=ALIGN)
            picked = entries(offs2_sb, half * BANK, (half + 1) * BANK)
            nc.vector.tensor_copy(planes[:], tab2_planes_raw[:].bitcast(U8).indirect(picked))
            return planes

        times_terrain(SLICES - 1)
        woven_x = [weave_x(1, n) for n in range(HALVES)]
        v2_codes = [gather_v2_words(keep, "last_terrain", 0)]
        v2_planes = [gather_v2_planes(keep, "wgs_rest", 0)]
        xq[1, 0] = quantise(woven_x[0], "x_codes10", "x_plane10")
        v2_planes.append(gather_v2_planes(ring, "woven", 1))
        xq[1, 1] = quantise(woven_x[1], "x_codes11", "x_plane11")
        v2_codes.append(gather_v2_words(ring, "woven", 1))

        def scores(i):
            e = row_tile()
            half, place_in_half = divmod(i, BANK // P)
            cols = slice(place_in_half * P, (place_in_half + 1) * P)
            for n in range(HALVES):
                bank = psum.tile([P, BANK], F32, name="score_bank", bufs=2 * HALVES)
                for a in range(PASSES):
                    codes, plane = xq[a, n]
                    nc.tensor.matmul_mx(
                        out=bank[:],
                        lhsT=v2_codes[half][:, a, cols].bitcast(FP8X4),
                        lhsT_scale=v2_planes[half][4 * a : P, cols],
                        rhs=codes[:].bitcast(FP8X4),
                        rhs_scale=plane[:],
                        start=(a == 0),
                        stop=(a == PASSES - 1),
                    )
                nc.scalar.copy(e[:, n * BANK : (n + 1) * BANK], bank[:])
            return e

        def pick(e, positions, lo, hi, name):
            picked = ring.tile([P, hi - lo], F32, name=name, bufs=3)
            nc.vector.tensor_copy(picked[:], e[:].indirect(entries(positions, lo, hi)))
            return picked

        def finish(i, lo, hi, head, tail):
            top = ring.tile([P, hi - lo], F32, name="top")
            nc.vector.tensor_tensor(top[:], head[:], tail[:], ALU.max)
            product = ring.tile([P, hi - lo], F32, name="product")
            engine = nc.vector if i == TILES - 1 else nc.gpsimd
            engine.tensor_tensor(product[:], top[:], head[:], ALU.mult)
            result = ring.tile([P, hi - lo], F32, name="result")
            nc.scalar.activation(result[:], product[:], ACT.Identity, bias=corridor_sb[:, i : i + 1])
            nc.sync.dma_start(out[i * P : (i + 1) * P, lo:hi], result[:])

        pieces = [(i, 0, PAIRS) for i in range(TILES - 1)]
        pieces = pieces + [(TILES - 1, 0, PAIRS // 2), (TILES - 1, PAIRS // 2, PAIRS)]
        e_tiles = {0: scores(0)}
        pending = None
        for i, lo, hi in pieces:
            if i + 1 < TILES:
                e_tiles[i + 1] = scores(i + 1)
            head = pick(e_tiles[i], pos1_sb, lo, hi, "head")
            if pending is not None:
                finish(*pending)
            pending = (i, lo, hi, head, pick(e_tiles[i], pos2_sb, lo, hi, "tail"))
        finish(*pending)
